import numpy as np
import ml_dtypes


def mxq(x, axis, fmt="e4m3"):
    dtype, down = {"e4m3": (ml_dtypes.float8_e4m3fn, 7), "e5m2": (ml_dtypes.float8_e5m2, 14)}[fmt]
    v = np.moveaxis(np.asarray(x, np.float32).astype(ml_dtypes.bfloat16).astype(np.float64), axis, -1)
    blocks = v.reshape(v.shape[:-1] + (-1, 32))
    amax = np.abs(blocks).max(-1, keepdims=True)
    byte = np.maximum(np.where(amax > 0, np.frexp(amax)[1] - 1 + 127, 0) - down, 1)
    scale = np.exp2(byte - 127.0)
    codes = (blocks / scale).astype(np.float32).astype(dtype).astype(np.float64)
    return np.moveaxis((codes * scale).reshape(v.shape), -1, axis)


WIDE = False


def mx_kscale(k):
    if not WIDE:
        return np.ones(k)
    levels = np.array([10, -10, 5, -5, 0])
    if k % 512:
        return np.exp2(np.random.permutation(np.resize(levels, k // 32))).repeat(32)
    a = np.empty((k // 512, 16))
    for p in range(k // 512):
        a[p, :8] = np.random.permutation(np.resize(levels, 8))
        for g in range(8):
            far = levels[np.abs(levels - a[p, g]) >= 10]
            a[p, g + 8] = far[np.random.randint(len(far))]
    return np.exp2(a.ravel()).repeat(32)


def f64(x):
    return np.asarray(x).astype(np.float64)


def striped(idx):
    return np.tile(idx.reshape(-1, 16).T, (8, 1)).astype(np.uint16)


def unstriped(offs):
    return offs[:16].T.reshape(-1).astype(np.int64)


E2M1 = np.array([0.0, 0.5, 1.0, 1.5, 2.0, 3.0, 4.0, 6.0, -0.0, -0.5, -1.0, -1.5, -2.0, -3.0, -4.0, -6.0])


def pack_weight(w, fmt):
    k, n = w.shape
    w = f64(np.asarray(w, np.float32).astype(ml_dtypes.bfloat16)).reshape(k // 32, 32, n)
    amax = np.abs(w).max(1)
    if fmt == "e4m3":
        byte = np.frexp(amax)[1] - 1 + 127 - 7
    else:
        mant, ex = np.frexp(amax / 6.0)
        byte = np.where(mant > 0.5, ex, ex - 1) + 127
    byte = np.clip(np.where(amax > 0, byte, 1), 1, 254)
    scaled = (w * np.exp2(127.0 - byte)[:, None, :]).reshape(k, n).astype(np.float32)
    by_word = np.ascontiguousarray(scaled.reshape(k // 512, 128, 4, n).transpose(0, 1, 3, 2))
    if fmt == "e4m3":
        words = by_word.astype(ml_dtypes.float8_e4m3fn).view(np.uint8)
    else:
        c = by_word.astype(ml_dtypes.float4_e2m1fn).view(np.uint8) & 0xF
        words = (c[..., 0::2] | (c[..., 1::2] << 4)).reshape(k // 512, 128, 2 * n)
    return np.ascontiguousarray(words), np.ascontiguousarray(byte.astype(np.uint8).reshape(k // 512, 16, n))


def unpack_weight(words, scales, fmt):
    g, _, n = scales.shape
    words = np.ascontiguousarray(words).reshape(g, 128, n, -1)
    if fmt == "e4m3":
        vals = words.view(ml_dtypes.float8_e4m3fn).astype(np.float64)
    else:
        nib = np.empty((g, 128, n, 4), np.uint8)
        nib[..., 0::2] = words & 0xF
        nib[..., 1::2] = words >> 4
        vals = E2M1[nib]
    vals = vals * np.repeat(np.exp2(scales.astype(np.float64) - 127.0), 8, axis=1)[..., None]
    return vals.transpose(0, 1, 3, 2).reshape(g * 512, n)


def relu2(v):
    return np.maximum(v, 0.0) ** 2


K, T, E, C, N = 512, 1536, 24, 128, 256


def by_expert(wq, xq):
    return np.concatenate([wq[e].T @ xq[:, e * C:(e + 1) * C] for e in range(E)], axis=1)


def setup_inputs():
    n = np.random.standard_normal
    s = mx_kscale(K)[:, None]
    first = np.random.permutation(np.repeat(np.arange(E), T // E))
    second = (first + 1 + np.random.permutation(np.repeat(np.arange(E - 1), -(-T // (E - 1)))[:T])) % E
    while np.bincount(second, minlength=E).max() != T // E:
        load = np.bincount(second, minlength=E); hi, lo = int(load.argmax()), int(load.argmin())
        t = np.flatnonzero((second == hi) & (first != lo))[0]; second[t] = lo
    slot_token = np.empty(E * C, np.int64); pos = np.empty((2, T), np.int64); fill = np.zeros(E, np.int64)
    place = np.stack([np.random.permutation(C) for _ in range(E)])
    for r, deal in enumerate((first, second)):
        for t in np.random.permutation(T):
            e = deal[t]; j = e * C + place[e, fill[e]]; fill[e] += 1; slot_token[j] = t; pos[r, t] = j
    g = np.random.uniform(0.2, 0.8, T)
    w = [pack_weight(m, "e2m1") for m in n((E, K, N)) / np.sqrt(K) / s[None]]
    return {
        "xT": (n((K, T)) * s).astype(np.float32),
        "w_words": np.stack([m[0] for m in w]),
        "w_scales": np.stack([m[1] for m in w]),
        "b": (0.3 * n((N, E))).astype(np.float32),
        "gate": np.stack([np.tile(g, (N, 1)), np.tile(1.0 - g, (N, 1))]).astype(np.float32),
        "offs": striped(slot_token),
        "pos1": striped(pos[0]),
        "pos2": striped(pos[1]),
    }


def reference(xT, w_words, w_scales, b, gate, offs, pos1, pos2):
    idx = unstriped(offs)
    w = np.stack([unpack_weight(w_words[e], w_scales[e], "e2m1") for e in range(E)])
    xq = mxq(f64(xT)[:, idx], 0, "e4m3")
    y = by_expert(w, xq)
    y = relu2(y + np.repeat(f64(b), C, axis=1))
    return f64(gate[0]) * y[:, unstriped(pos1)] + f64(gate[1]) * y[:, unstriped(pos2)]

@@ -1,0 +1,153 @@
+from contextlib import ExitStack
+
+import concourse.mybir as mybir
+
+K, T, E, C, N = 512, 1536, 24, 128, 256
+S = E * C
+P = 128
+FLOPS = 2 * K * N * S
+
+F32 = mybir.dt.float32
+BF16 = mybir.dt.bfloat16
+I32 = mybir.dt.int32
+U32 = mybir.dt.uint32
+U16 = mybir.dt.uint16
+U8 = mybir.dt.uint8
+FP8X4 = mybir.dt.float8_e4m3fn_x4
+FP4X4 = mybir.dt.float4_e2m1fn_x4
+ACT = mybir.ActivationFunctionType
+MULT = mybir.AluOpType.mult
+MAX = mybir.AluOpType.max
+ADD = mybir.AluOpType.add
+
+X_CHUNKS = ((0, 768), (768, 512), (1280, 256))
+Q_CHUNKS = ((0, 0, 512, 224), (0, 512, 256, 112), (1, 768, 512, 224), (2, 1280, 256, 144))
+E_CHUNKS = ((0, 4), (4, 8), (8, 12), (12, 16), (16, 20), (20, 22), (22, 24))
+PIECES = ((0, 0, 1536), (1, 0, 1024), (1, 1024, 1344), (1, 1344, 1536))
+
+
+def tile_moe_pln_lin_relu2_kernel(tc, xT, w_words, w_scales, b, gate, offs, pos1, pos2, out):
+    nc = tc.nc
+    with ExitStack() as ctx:
+        held = ctx.enter_context(tc.tile_pool(name="held", bufs=1))
+        xpool = ctx.enter_context(tc.tile_pool(name="xpool", bufs=1))
+        rpool = ctx.enter_context(tc.tile_pool(name="rpool", bufs=3))
+        opool = ctx.enter_context(tc.tile_pool(name="opool", bufs=1))
+        psum = ctx.enter_context(tc.psum_pool(name="psum", bufs=4))
+
+        offs_t = held.tile([P, S // 16], U16, name="offs_t")
+        pos1_t = held.tile([P, T // 16], U16, name="pos1_t")
+        pos2_t = held.tile([P, T // 16], U16, name="pos2_t")
+        words = held.tile([P, T], U32, name="words", align_bytes=64)
+        sbytes = held.tile([P, T], U8, name="sbytes", align_bytes=64)
+        slot_words = held.tile([P, S], U32, name="slot_words", align_bytes=64)
+        slot_bytes = held.tile([P, S], U8, name="slot_bytes", align_bytes=64)
+        w_t = held.tile([P, E, 2 * N], U8, name="w_t", align_bytes=64)
+        w_sc = held.tile([P, E * N], U8, name="w_sc", align_bytes=64)
+        b_t = held.tile([P, 2, E], F32, name="b_t")
+        y_t = [held.tile([P, S], F32, name=f"y{h}") for h in range(2)]
+        g_t = [[held.tile([P, T], F32, name=f"g{i}{h}") for h in range(2)] for i in range(2)]
+
+        nc.vector.memset(w_sc[:].bitcast(I32), 0)
+        nc.gpsimd.memset(sbytes[:], 0)
+
+        x_view = xT.rearrange("(p j) w -> p j w", j=4)
+        raws = []
+        for i, (t0, width) in enumerate(X_CHUNKS):
+            raw = xpool.tile([P, 4, width], F32, name=f"raw{i}")
+            nc.sync.dma_start(out=raw[:], in_=x_view[:, :, t0 : t0 + width])
+            raws.append(raw)
+        nc.sync.dma_start(offs_t[:], offs)
+        nc.sync.dma_start(out=b_t[:], in_=b.rearrange("(h p) e -> p h e", p=P))
+        w_view = w_words.rearrange("e a p c -> p (e a) c")
+
+        def load_w(e0, e1):
+            nc.sync.dma_start(out=w_t[:, e0:e1, :].bitcast(I32), in_=w_view[:, e0:e1, :].bitcast(I32))
+
+        load_w(0, 8)
+        sc_view = w_scales.rearrange("e a q n -> q (e a) n")
+        w_sc3 = w_sc[:].rearrange("p (e n) -> p e n", n=N)
+        for q in range(4):
+            nc.sync.dma_start(
+                out=w_sc3[32 * q : 32 * q + 4, :, :].bitcast(I32),
+                in_=sc_view[4 * q : 4 * q + 4, :, :].bitcast(I32),
+            )
+        load_w(8, 16)
+        load_w(16, 24)
+        nc.sync.dma_start(pos1_t[:], pos1)
+        nc.sync.dma_start(pos2_t[:], pos2)
+        for h in range(2):
+            for i in range(2):
+                nc.sync.dma_start(out=g_t[i][h][:], in_=gate[i, h * P : (h + 1) * P, :])
+
+        for i, (chunk, t0, width, cut) in enumerate(Q_CHUNKS):
+            grouped = xpool.tile([P, width, 4], BF16, name=f"grouped{i}", align_bytes=64)
+            at = t0 - X_CHUNKS[chunk][0]
+            src = raws[chunk][:, :, at : at + width].rearrange("p j w -> p w j")
+            nc.vector.tensor_copy(out=grouped[:, :cut, :], in_=src[:, :cut, :])
+            nc.scalar.copy(out=grouped[:, cut:, :], in_=src[:, cut:, :])
+            nc.vector.quantize_mx(
+                out=words[:, t0 : t0 + width].bitcast(FP8X4),
+                scales=sbytes[:, t0 : t0 + width],
+                in_=grouped[:].rearrange("p w j -> p (w j)"),
+            )
+
+        for e0, e1 in E_CHUNKS:
+            lo, hi = e0 * C, e1 * C
+            cols = offs_t[:, lo // 16 : hi // 16]
+            nc.vector.tensor_copy(slot_words[:, lo:hi], words[:].indirect(cols))
+            nc.vector.tensor_copy(slot_bytes[:, lo:hi], sbytes[:].indirect(cols))
+
+        def product(acc, e, h):
+            nc.tensor.matmul_mx(
+                out=acc,
+                lhsT=w_t[:, e, h * N : (h + 1) * N].bitcast(FP4X4),
+                lhsT_scale=w_sc[:, e * N + h * P : e * N + (h + 1) * P],
+                rhs=slot_words[:, e * C : (e + 1) * C].bitcast(FP8X4),
+                rhs_scale=slot_bytes[:, e * C : (e + 1) * C],
+                start=True,
+                stop=True,
+            )
+
+        for h in range(2):
+            for e0, e1 in E_CHUNKS:
+                width = (e1 - e0) * C
+                if h == 0 and e1 == E:
+                    accs = []
+                    for e in range(e0, e1):
+                        acc = psum.tile([P, 512], F32, name="acc0")
+                        product(acc[:, :C], e, h)
+                        accs.append(acc)
+                    r = rpool.tile([P, C], F32, name="rs")
+                    nc.scalar.activation(r[:], accs[0][:, :C], ACT.Relu, bias=b_t[:, h, e0 : e0 + 1])
+                    r2 = rpool.tile([P, C], F32, name="rv")
+                    nc.vector.tensor_scalar(r2[:], accs[1][:, :C], b_t[:, h, e0 + 1 : e1], 0.0, ADD, MAX)
+                    nc.scalar.activation(y_t[h][:, e0 * C : (e0 + 1) * C], r[:], ACT.Square)
+                    nc.vector.tensor_tensor(y_t[h][:, (e0 + 1) * C : e1 * C], r2[:], r2[:], MULT)
+                    continue
+                acc = psum.tile([P, 512], F32, name=f"acc{h}")
+                for e in range(e0, e1):
+                    m = slice((e - e0) * C, (e - e0 + 1) * C)
+                    product(acc[:, m], e, h)
+                r = rpool.tile([P, 512], F32, name=f"r{h}")
+                for e in range(e0, e1):
+                    m = slice((e - e0) * C, (e - e0 + 1) * C)
+                    nc.scalar.activation(r[:, m], acc[:, m], ACT.Relu, bias=b_t[:, h, e : e + 1])
+                nc.scalar.activation(y_t[h][:, e0 * C : e1 * C], r[:, :width], ACT.Square)
+
+        def finish(piece):
+            h, t0, t1, a, d = piece
+            nc.vector.tensor_tensor(a[:], a[:], d[:], ADD)
+            nc.sync.dma_start(out=out[h * P : (h + 1) * P, t0:t1], in_=a[:])
+
+        pending = None
+        for h, t0, t1 in PIECES:
+            n = t1 - t0
+            a = opool.tile([P, n], F32, name=f"a{h}{t0}")
+            d = opool.tile([P, n], F32, name=f"d{h}{t0}")
+            nc.vector.tensor_tensor(a[:], y_t[h][:].indirect(pos1_t[:, t0 // 16 : t1 // 16]), g_t[0][h][:, t0:t1], MULT)
+            if pending:
+                finish(pending)
+            nc.vector.tensor_tensor(d[:], y_t[h][:].indirect(pos2_t[:, t0 // 16 : t1 // 16]), g_t[1][h][:, t0:t1], MULT)
+            pending = (h, t0, t1, a, d)
+        finish(pending)

@@ -21,9 +21,10 @@ MAX = mybir.AluOpType.max
 ADD = mybir.AluOpType.add
 
 X_CHUNKS = ((0, 768), (768, 512), (1280, 256))
-Q_CHUNKS = ((0, 0, 512, 224), (0, 512, 256, 112), (1, 768, 512, 224), (2, 1280, 256, 144))
+Q_CHUNKS = ((0, 0, 512, 224), (0, 512, 256, 112), (1, 768, 512, 288), (2, 1280, 256, 160))
+G_CHUNKS = ((0, 4), (4, 8), (8, 12), (12, 16), (16, 20), (20, 22), (22, 24))
 E_CHUNKS = ((0, 4), (4, 8), (8, 12), (12, 16), (16, 20), (20, 22), (22, 24))
-PIECES = ((0, 0, 1536), (1, 0, 1024), (1, 1024, 1344), (1, 1344, 1536))
+PIECES = ((0, 0, 768), (0, 768, 1536), (1, 0, 1024), (1, 1024, 1280), (1, 1280, 1536))
 
 
 def tile_moe_pln_lin_relu2_kernel(tc, xT, w_words, w_scales, b, gate, offs, pos1, pos2, out):
@@ -57,14 +58,13 @@ def tile_moe_pln_lin_relu2_kernel(tc, xT, w_words, w_scales, b, gate, offs, pos1
             raw = xpool.tile([P, 4, width], F32, name=f"raw{i}")
             nc.sync.dma_start(out=raw[:], in_=x_view[:, :, t0 : t0 + width])
             raws.append(raw)
-        nc.sync.dma_start(offs_t[:], offs)
-        nc.sync.dma_start(out=b_t[:], in_=b.rearrange("(h p) e -> p h e", p=P))
+            if i == 1:
+                nc.sync.dma_start(offs_t[:], offs)
         w_view = w_words.rearrange("e a p c -> p (e a) c")
 
         def load_w(e0, e1):
             nc.sync.dma_start(out=w_t[:, e0:e1, :].bitcast(I32), in_=w_view[:, e0:e1, :].bitcast(I32))
 
-        load_w(0, 8)
         sc_view = w_scales.rearrange("e a q n -> q (e a) n")
         w_sc3 = w_sc[:].rearrange("p (e n) -> p e n", n=N)
         for q in range(4):
@@ -72,6 +72,8 @@ def tile_moe_pln_lin_relu2_kernel(tc, xT, w_words, w_scales, b, gate, offs, pos1
                 out=w_sc3[32 * q : 32 * q + 4, :, :].bitcast(I32),
                 in_=sc_view[4 * q : 4 * q + 4, :, :].bitcast(I32),
             )
+        nc.sync.dma_start(out=b_t[:], in_=b.rearrange("(h p) e -> p h e", p=P))
+        load_w(0, 8)
         load_w(8, 16)
         load_w(16, 24)
         nc.sync.dma_start(pos1_t[:], pos1)
@@ -83,16 +85,17 @@ def tile_moe_pln_lin_relu2_kernel(tc, xT, w_words, w_scales, b, gate, offs, pos1
         for i, (chunk, t0, width, cut) in enumerate(Q_CHUNKS):
             grouped = xpool.tile([P, width, 4], BF16, name=f"grouped{i}", align_bytes=64)
             at = t0 - X_CHUNKS[chunk][0]
-            src = raws[chunk][:, :, at : at + width].rearrange("p j w -> p w j")
-            nc.vector.tensor_copy(out=grouped[:, :cut, :], in_=src[:, :cut, :])
-            nc.scalar.copy(out=grouped[:, cut:, :], in_=src[:, cut:, :])
+            src = raws[chunk][:, :, at : at + width].rearrange("p j (c i) -> p c j i", i=4)
+            dst = grouped[:].rearrange("p (c i) j -> p c j i", i=4)
+            nc.vector.tensor_copy(out=dst[:, : cut // 4], in_=src[:, : cut // 4])
+            nc.scalar.copy(out=dst[:, cut // 4 :], in_=src[:, cut // 4 :])
             nc.vector.quantize_mx(
                 out=words[:, t0 : t0 + width].bitcast(FP8X4),
                 scales=sbytes[:, t0 : t0 + width],
                 in_=grouped[:].rearrange("p w j -> p (w j)"),
             )
 
-        for e0, e1 in E_CHUNKS:
+        for e0, e1 in G_CHUNKS:
             lo, hi = e0 * C, e1 * C
             cols = offs_t[:, lo // 16 : hi // 16]
             nc.vector.tensor_copy(slot_words[:, lo:hi], words[:].indirect(cols))
@@ -135,19 +138,36 @@ def tile_moe_pln_lin_relu2_kernel(tc, xT, w_words, w_scales, b, gate, offs, pos1
                     nc.scalar.activation(r[:, m], acc[:, m], ACT.Relu, bias=b_t[:, h, e : e + 1])
                 nc.scalar.activation(y_t[h][:, e0 * C : e1 * C], r[:, :width], ACT.Square)
 
-        def finish(piece):
-            h, t0, t1, a, d = piece
+        def first(piece):
+            h, t0, t1 = piece
+            a = opool.tile([P, t1 - t0], F32, name=f"a{h}{t0}")
+            nc.vector.tensor_tensor(a[:], y_t[h][:].indirect(pos1_t[:, t0 // 16 : t1 // 16]), g_t[0][h][:, t0:t1], MULT)
+            return a
+
+        def second(piece):
+            h, t0, t1 = piece
+            d = opool.tile([P, t1 - t0], F32, name=f"d{h}{t0}")
+            nc.vector.tensor_tensor(d[:], y_t[h][:].indirect(pos2_t[:, t0 // 16 : t1 // 16]), g_t[1][h][:, t0:t1], MULT)
+            return d
+
+        def finish(piece, a, d):
+            h, t0, t1 = piece
             nc.vector.tensor_tensor(a[:], a[:], d[:], ADD)
             nc.sync.dma_start(out=out[h * P : (h + 1) * P, t0:t1], in_=a[:])
 
-        pending = None
-        for h, t0, t1 in PIECES:
-            n = t1 - t0
-            a = opool.tile([P, n], F32, name=f"a{h}{t0}")
-            d = opool.tile([P, n], F32, name=f"d{h}{t0}")
-            nc.vector.tensor_tensor(a[:], y_t[h][:].indirect(pos1_t[:, t0 // 16 : t1 // 16]), g_t[0][h][:, t0:t1], MULT)
-            if pending:
-                finish(pending)
-            nc.vector.tensor_tensor(d[:], y_t[h][:].indirect(pos2_t[:, t0 // 16 : t1 // 16]), g_t[1][h][:, t0:t1], MULT)
-            pending = (h, t0, t1, a, d)
-        finish(pending)
+        p0, p1, p2, p3, p4 = PIECES
+        a0 = first(p0)
+        a1 = first(p1)
+        d0 = second(p0)
+        d1 = second(p1)
+        finish(p0, a0, d0)
+        finish(p1, a1, d1)
+        a2 = first(p2)
+        d2 = second(p2)
+        a3 = first(p3)
+        finish(p2, a2, d2)
+        d3 = second(p3)
+        a4 = first(p4)
+        d4 = second(p4)
+        finish(p3, a3, d3)
+        finish(p4, a4, d4)

from contextlib import ExitStack

import concourse.mybir as mybir

K, T, E, C, N = 512, 1536, 24, 128, 256
S = E * C
P = 128
FLOPS = 2 * K * N * S

F32 = mybir.dt.float32
BF16 = mybir.dt.bfloat16
I32 = mybir.dt.int32
U32 = mybir.dt.uint32
U16 = mybir.dt.uint16
U8 = mybir.dt.uint8
FP8X4 = mybir.dt.float8_e4m3fn_x4
FP4X4 = mybir.dt.float4_e2m1fn_x4
ACT = mybir.ActivationFunctionType
MULT = mybir.AluOpType.mult
MAX = mybir.AluOpType.max
ADD = mybir.AluOpType.add

X_CHUNKS = ((0, 768), (768, 512), (1280, 256))
Q_CHUNKS = ((0, 0, 512, 224), (0, 512, 256, 112), (1, 768, 512, 288), (2, 1280, 256, 160))
G_CHUNKS = ((0, 4), (4, 8), (8, 12), (12, 16), (16, 20), (20, 22), (22, 24))
E_CHUNKS = ((0, 4), (4, 8), (8, 12), (12, 16), (16, 20), (20, 22), (22, 24))
PIECES = ((0, 0, 768), (0, 768, 1536), (1, 0, 1024), (1, 1024, 1280), (1, 1280, 1536))


def tile_moe_pln_lin_relu2_kernel(tc, xT, w_words, w_scales, b, gate, offs, pos1, pos2, out):
    nc = tc.nc
    with ExitStack() as ctx:
        held = ctx.enter_context(tc.tile_pool(name="held", bufs=1))
        xpool = ctx.enter_context(tc.tile_pool(name="xpool", bufs=1))
        rpool = ctx.enter_context(tc.tile_pool(name="rpool", bufs=3))
        opool = ctx.enter_context(tc.tile_pool(name="opool", bufs=1))
        psum = ctx.enter_context(tc.psum_pool(name="psum", bufs=4))

        offs_t = held.tile([P, S // 16], U16, name="offs_t")
        pos1_t = held.tile([P, T // 16], U16, name="pos1_t")
        pos2_t = held.tile([P, T // 16], U16, name="pos2_t")
        words = held.tile([P, T], U32, name="words", align_bytes=64)
        sbytes = held.tile([P, T], U8, name="sbytes", align_bytes=64)
        slot_words = held.tile([P, S], U32, name="slot_words", align_bytes=64)
        slot_bytes = held.tile([P, S], U8, name="slot_bytes", align_bytes=64)
        w_t = held.tile([P, E, 2 * N], U8, name="w_t", align_bytes=64)
        w_sc = held.tile([P, E * N], U8, name="w_sc", align_bytes=64)
        b_t = held.tile([P, 2, E], F32, name="b_t")
        y_t = [held.tile([P, S], F32, name=f"y{h}") for h in range(2)]
        g_t = [[held.tile([P, T], F32, name=f"g{i}{h}") for h in range(2)] for i in range(2)]

        nc.vector.memset(w_sc[:].bitcast(I32), 0)
        nc.gpsimd.memset(sbytes[:], 0)

        x_view = xT.rearrange("(p j) w -> p j w", j=4)
        raws = []
        for i, (t0, width) in enumerate(X_CHUNKS):
            raw = xpool.tile([P, 4, width], F32, name=f"raw{i}")
            nc.sync.dma_start(out=raw[:], in_=x_view[:, :, t0 : t0 + width])
            raws.append(raw)
            if i == 1:
                nc.sync.dma_start(offs_t[:], offs)
        w_view = w_words.rearrange("e a p c -> p (e a) c")

        def load_w(e0, e1):
            nc.sync.dma_start(out=w_t[:, e0:e1, :].bitcast(I32), in_=w_view[:, e0:e1, :].bitcast(I32))

        sc_view = w_scales.rearrange("e a q n -> q (e a) n")
        w_sc3 = w_sc[:].rearrange("p (e n) -> p e n", n=N)
        for q in range(4):
            nc.sync.dma_start(
                out=w_sc3[32 * q : 32 * q + 4, :, :].bitcast(I32),
                in_=sc_view[4 * q : 4 * q + 4, :, :].bitcast(I32),
            )
        nc.sync.dma_start(out=b_t[:], in_=b.rearrange("(h p) e -> p h e", p=P))
        load_w(0, 8)
        load_w(8, 16)
        load_w(16, 24)
        nc.sync.dma_start(pos1_t[:], pos1)
        nc.sync.dma_start(pos2_t[:], pos2)
        for h in range(2):
            for i in range(2):
                nc.sync.dma_start(out=g_t[i][h][:], in_=gate[i, h * P : (h + 1) * P, :])

        for i, (chunk, t0, width, cut) in enumerate(Q_CHUNKS):
            grouped = xpool.tile([P, width, 4], BF16, name=f"grouped{i}", align_bytes=64)
            at = t0 - X_CHUNKS[chunk][0]
            src = raws[chunk][:, :, at : at + width].rearrange("p j (c i) -> p c j i", i=4)
            dst = grouped[:].rearrange("p (c i) j -> p c j i", i=4)
            nc.vector.tensor_copy(out=dst[:, : cut // 4], in_=src[:, : cut // 4])
            nc.scalar.copy(out=dst[:, cut // 4 :], in_=src[:, cut // 4 :])
            nc.vector.quantize_mx(
                out=words[:, t0 : t0 + width].bitcast(FP8X4),
                scales=sbytes[:, t0 : t0 + width],
                in_=grouped[:].rearrange("p w j -> p (w j)"),
            )

        for e0, e1 in G_CHUNKS:
            lo, hi = e0 * C, e1 * C
            cols = offs_t[:, lo // 16 : hi // 16]
            nc.vector.tensor_copy(slot_words[:, lo:hi], words[:].indirect(cols))
            nc.vector.tensor_copy(slot_bytes[:, lo:hi], sbytes[:].indirect(cols))

        def product(acc, e, h):
            nc.tensor.matmul_mx(
                out=acc,
                lhsT=w_t[:, e, h * N : (h + 1) * N].bitcast(FP4X4),
                lhsT_scale=w_sc[:, e * N + h * P : e * N + (h + 1) * P],
                rhs=slot_words[:, e * C : (e + 1) * C].bitcast(FP8X4),
                rhs_scale=slot_bytes[:, e * C : (e + 1) * C],
                start=True,
                stop=True,
            )

        for h in range(2):
            for e0, e1 in E_CHUNKS:
                width = (e1 - e0) * C
                if h == 0 and e1 == E:
                    accs = []
                    for e in range(e0, e1):
                        acc = psum.tile([P, 512], F32, name="acc0")
                        product(acc[:, :C], e, h)
                        accs.append(acc)
                    r = rpool.tile([P, C], F32, name="rs")
                    nc.scalar.activation(r[:], accs[0][:, :C], ACT.Relu, bias=b_t[:, h, e0 : e0 + 1])
                    r2 = rpool.tile([P, C], F32, name="rv")
                    nc.vector.tensor_scalar(r2[:], accs[1][:, :C], b_t[:, h, e0 + 1 : e1], 0.0, ADD, MAX)
                    nc.scalar.activation(y_t[h][:, e0 * C : (e0 + 1) * C], r[:], ACT.Square)
                    nc.vector.tensor_tensor(y_t[h][:, (e0 + 1) * C : e1 * C], r2[:], r2[:], MULT)
                    continue
                acc = psum.tile([P, 512], F32, name=f"acc{h}")
                for e in range(e0, e1):
                    m = slice((e - e0) * C, (e - e0 + 1) * C)
                    product(acc[:, m], e, h)
                r = rpool.tile([P, 512], F32, name=f"r{h}")
                for e in range(e0, e1):
                    m = slice((e - e0) * C, (e - e0 + 1) * C)
                    nc.scalar.activation(r[:, m], acc[:, m], ACT.Relu, bias=b_t[:, h, e : e + 1])
                nc.scalar.activation(y_t[h][:, e0 * C : e1 * C], r[:, :width], ACT.Square)

        def first(piece):
            h, t0, t1 = piece
            a = opool.tile([P, t1 - t0], F32, name=f"a{h}{t0}")
            nc.vector.tensor_tensor(a[:], y_t[h][:].indirect(pos1_t[:, t0 // 16 : t1 // 16]), g_t[0][h][:, t0:t1], MULT)
            return a

        def second(piece):
            h, t0, t1 = piece
            d = opool.tile([P, t1 - t0], F32, name=f"d{h}{t0}")
            nc.vector.tensor_tensor(d[:], y_t[h][:].indirect(pos2_t[:, t0 // 16 : t1 // 16]), g_t[1][h][:, t0:t1], MULT)
            return d

        def finish(piece, a, d):
            h, t0, t1 = piece
            nc.vector.tensor_tensor(a[:], a[:], d[:], ADD)
            nc.sync.dma_start(out=out[h * P : (h + 1) * P, t0:t1], in_=a[:])

        p0, p1, p2, p3, p4 = PIECES
        a0 = first(p0)
        a1 = first(p1)
        d0 = second(p0)
        d1 = second(p1)
        finish(p0, a0, d0)
        finish(p1, a1, d1)
        a2 = first(p2)
        d2 = second(p2)
        a3 = first(p3)
        finish(p2, a2, d2)
        d3 = second(p3)
        a4 = first(p4)
        d4 = second(p4)
        finish(p3, a3, d3)
        finish(p4, a4, d4)
